import numpy as np
import ml_dtypes


def mxq(x, axis, fmt="e4m3"):
    dtype, down = {"e4m3": (ml_dtypes.float8_e4m3fn, 7), "e5m2": (ml_dtypes.float8_e5m2, 14)}[fmt]
    v = np.moveaxis(np.asarray(x, np.float32).astype(ml_dtypes.bfloat16).astype(np.float64), axis, -1)
    blocks = v.reshape(v.shape[:-1] + (-1, 32))
    amax = np.abs(blocks).max(-1, keepdims=True)
    byte = np.maximum(np.where(amax > 0, np.frexp(amax)[1] - 1 + 127, 0) - down, 1)
    scale = np.exp2(byte - 127.0)
    codes = (blocks / scale).astype(np.float32).astype(dtype).astype(np.float64)
    return np.moveaxis((codes * scale).reshape(v.shape), -1, axis)


WIDE = False


def mx_kscale(k):
    if not WIDE:
        return np.ones(k)
    levels = np.array([10, -10, 5, -5, 0])
    if k % 512:
        return np.exp2(np.random.permutation(np.resize(levels, k // 32))).repeat(32)
    a = np.empty((k // 512, 16))
    for p in range(k // 512):
        a[p, :8] = np.random.permutation(np.resize(levels, 8))
        for g in range(8):
            far = levels[np.abs(levels - a[p, g]) >= 10]
            a[p, g + 8] = far[np.random.randint(len(far))]
    return np.exp2(a.ravel()).repeat(32)


def f64(x):
    return np.asarray(x).astype(np.float64)


def striped(idx):
    return np.tile(idx.reshape(-1, 16).T, (8, 1)).astype(np.uint16)


def unstriped(offs):
    return offs[:16].T.reshape(-1).astype(np.int64)


def striped8(idx):
    return np.concatenate([x.reshape(-1, 16).T for x in idx]).astype(np.uint16)


def runs(offs, k):
    lists = np.stack([offs[16 * r : 16 * r + 16].T.reshape(-1) for r in range(8)]).astype(np.int64)
    return lists[np.arange(k) % 512 // 64]


def pack_weight(w):
    k, n = w.shape
    w = f64(np.asarray(w, np.float32).astype(ml_dtypes.bfloat16)).reshape(k // 32, 32, n)
    amax = np.abs(w).max(1)
    byte = np.clip(np.where(amax > 0, np.frexp(amax)[1] - 1 + 127 - 7, 1), 1, 254)
    scaled = (w * np.exp2(127.0 - byte)[:, None, :]).reshape(k, n).astype(np.float32)
    words = np.ascontiguousarray(scaled.reshape(k // 512, 128, 4, n).transpose(0, 1, 3, 2)).astype(ml_dtypes.float8_e4m3fn).view(np.uint8)
    return words, np.ascontiguousarray(byte.astype(np.uint8).reshape(k // 512, 16, n))


def unpack_weight(words, scales):
    g, p, n, _ = words.shape
    vals = np.ascontiguousarray(words).view(ml_dtypes.float8_e4m3fn).astype(np.float64) * np.repeat(np.exp2(scales.astype(np.float64) - 127.0), 8, axis=1)[..., None]
    return vals.transpose(0, 1, 3, 2).reshape(g * 512, n)


def relu(v):
    return np.maximum(v, 0.0)


K, T, S, G, H, U, C = 512, 1024, 512, 2048, 512, 1024, 512


def setup_inputs():
    n = np.random.standard_normal
    s = mx_kscale(K)[:, None]
    packed_xT = pack_weight(n((K, T)) * s)
    packed_dT = pack_weight(n((K, G)) / s)
    return {
        "x_words": packed_xT[0],
        "x_scales": packed_xT[1],
        "d_words": packed_dT[0],
        "d_scales": packed_dT[1],
        "mem": n((H, U)).astype(np.float32),
        "gs": (np.random.uniform(0.5, 1.5, (K, 1)) / s).astype(np.float32),
        "offs": striped(np.random.permutation(T)[:S]),
        "k1": striped8(np.random.randint(0, G, (8, H))),
        "n1": striped8(np.stack([np.random.permutation(U)[:S] for _ in range(8)])),
        "n2": striped8(np.stack([np.random.permutation(U) for _ in range(8)])),
        "cand": striped(np.random.permutation(T)[:C]),
        "n3": striped8(np.stack([np.random.permutation(U) for _ in range(8)])),
    }


def reference(x_words, x_scales, d_words, d_scales, mem, gs, offs, k1, n1, n2, cand, n3):
    x_cand = unpack_weight(x_words, x_scales)[:, unstriped(cand)]
    d_k1 = unpack_weight(d_words, d_scales)[np.arange(K)[:, None], runs(k1, K)]
    xq = unpack_weight(x_words, x_scales)[:, unstriped(offs)]
    h = 0.0625 * (d_k1.T @ xq)
    pg = f64(mem).copy()
    pg[np.arange(H)[:, None], runs(n1, H)] = h
    z = f64(gs) * (pg - (0.5 * (pg[np.arange(H)[:, None], runs(n2, H)])))
    s = 0.0625 * ((x_cand.T @ mxq(z, 0, "e4m3")))
    rl = relu(s)
    ds = np.zeros((C, U))
    ds[np.arange(C)[:, None], runs(n3, C)] = rl
    return ds - (0.5 * s)

@@ -1,0 +1,175 @@
+from contextlib import ExitStack
+
+import concourse.mybir as mybir
+
+F32 = mybir.dt.float32
+BF16 = mybir.dt.bfloat16
+I32 = mybir.dt.int32
+U32 = mybir.dt.uint32
+U16 = mybir.dt.uint16
+U8 = mybir.dt.uint8
+FP8X4 = mybir.dt.float8_e4m3fn_x4
+ALU = mybir.AluOpType
+ACT = mybir.ActivationFunctionType
+
+P = 128
+PACK = 4
+K, T, S, G, H, U, C = 512, 1024, 512, 2048, 512, 1024, 512
+BANK = 512
+FLOPS = 2 * K * H * S + 2 * K * C * U
+
+
+def deal(nc, out, in_):
+    nc.vector.tensor_copy(out=out.rearrange("p (t m) -> p t m", t=PACK), in_=in_.rearrange("p (m t) -> p t m", t=PACK))
+
+
+def interleave(nc, out, in_):
+    nc.scalar.copy(out=out.rearrange("p (c i) t -> p c t i", i=4), in_=in_.rearrange("p t (c i) -> p c t i", i=4))
+
+
+def tile_picked_pqcpagemsend_none_p_kernel(tc, x_words, x_scales, d_words, d_scales, mem, gs, offs, k1, n1, n2, cand, n3, out):
+    nc = tc.nc
+    with ExitStack() as ctx:
+        lists = ctx.enter_context(tc.tile_pool(name="lists", bufs=1))
+        sb = ctx.enter_context(tc.tile_pool(name="sb", bufs=1))
+        psum = ctx.enter_context(tc.psum_pool(name="psum", bufs=1))
+
+        def tile(name, shape, dtype, tag=None):
+            return sb.tile(shape, dtype, name=name, tag=tag or name, align_bytes=64)
+
+        def load_list(name, src):
+            t = lists.tile(list(src.shape), U16, name=name)
+            nc.sync.dma_start(t[:], src)
+            return t
+
+        mem_rows = mem.rearrange("(p t) w -> t p w", t=PACK)
+        out_rows = out.rearrange("(p t) w -> t p w", t=PACK)
+
+        d_bytes = tile("d_bytes", [P, G], U8)
+        x_bytes = tile("x_bytes", [P, T], U8)
+        nc.vector.memset(d_bytes[:].bitcast(I32), 0)
+        nc.gpsimd.memset(x_bytes[:].bitcast(I32), 0)
+        offs_t = load_list("offs_t", offs)
+        x_tab = tile("x_tab", [P, T], U32)
+        nc.sync.dma_start(x_tab[:].bitcast(I32), x_words[0].rearrange("p n t -> p (n t)").bitcast(I32))
+        k1_t = load_list("k1_t", k1)
+        for j in range(2):
+            nc.scalar.dma_start(d_bytes[j:P:16, :].bitcast(I32), d_scales[0, j:16:2, :].bitcast(I32))
+        cand_t = load_list("cand_t", cand)
+        n1_t = load_list("n1_t", n1)
+        d_tab = tile("d_tab", [P, G], U32)
+        nc.sync.dma_start(d_tab[:].bitcast(I32), d_words[0].rearrange("p n t -> p (n t)").bitcast(I32))
+        for q in range(4):
+            nc.sync.dma_start(x_bytes[32 * q : 32 * q + 4, :].bitcast(I32), x_scales[0, 4 * q : 4 * q + 4, :].bitcast(I32))
+        pg = [tile("pg0", [P, U], F32)]
+        nc.sync.dma_start(pg[0][:], mem_rows[0])
+        gain = tile("gain", [P, PACK], F32)
+        nc.sync.dma_start(gain[:], gs.rearrange("(p t) o -> p (t o)", t=PACK))
+        n2_t = load_list("n2_t", n2)
+        n3_t = load_list("n3_t", n3)
+
+        xw = tile("xw", [P, S], U32)
+        nc.vector.tensor_copy(out=xw[:], in_=x_tab[:].indirect(offs_t[:]))
+        db_picked = tile("db_picked", [P, H], U8, tag="slot1")
+        nc.vector.tensor_copy(out=db_picked[:], in_=d_bytes[:].indirect(k1_t[:]))
+        db = tile("db", [P, H], U8)
+        deal(nc, db[:], db_picked[:])
+        for j in range(2):
+            nc.scalar.dma_start(db[2 + j : P : 32, :].bitcast(I32), db[16 + j : P : 32, :].bitcast(I32))
+        dw_picked = tile("dw_picked", [P, H], U32, tag="slot3")
+        nc.vector.tensor_copy(out=dw_picked[:], in_=d_tab[:].indirect(k1_t[:]))
+        dw = tile("dw", [P, H], U32)
+        deal(nc, dw[:], dw_picked[:])
+        xb = tile("xb", [P, S], U8)
+        nc.vector.tensor_copy(out=xb[:], in_=x_bytes[:].indirect(offs_t[:]))
+        cw_picked = tile("cw_picked", [P, C], U32)
+        nc.vector.tensor_copy(out=cw_picked[:], in_=x_tab[:].indirect(cand_t[:]))
+        cw = tile("cw", [P, C], U32)
+        deal(nc, cw[:], cw_picked[:])
+
+        for t, tag in ((1, "slot1"), (2, "d_tab"), (3, "slot3")):
+            pg.append(tile(f"pg{t}", [P, U], F32, tag=tag))
+            nc.sync.dma_start(pg[t][:], mem_rows[t])
+
+        half_gain = tile("half_gain", [P, PACK], F32)
+        nc.scalar.activation(half_gain[:], gain[:], ACT.Copy, scale=-0.5)
+
+        for t in range(PACK):
+            cols = slice(t * P, (t + 1) * P)
+            acc = psum.tile([P, S], F32, name=f"h_acc{t}", tag=f"bank{t}")
+            nc.tensor.matmul_mx(acc[:], lhsT=dw[:, cols].bitcast(FP8X4), lhsT_scale=db[:, cols],
+                                rhs=xw[:].bitcast(FP8X4), rhs_scale=xb[:], start=True, stop=True)
+            h = tile(f"h{t}", [P, S], F32)
+            nc.scalar.activation(h[:], acc[:], ACT.Copy, scale=0.0625)
+            nc.vector.tensor_copy(out=pg[t][:].indirect(n1_t[:]), in_=h[:])
+
+        own, other = [], []
+        za = tile("za", [P, PACK, BANK], F32)
+
+        def z_piece(dst, t, w0, w1):
+            nc.vector.tensor_tensor(dst[:, t, :], other[t][:].indirect(n2_t[:, w0 // 16 : w1 // 16]), own[t][:, w0:w1], ALU.add)
+
+        for t in range(PACK):
+            other.append(tile(f"other{t}", [P, U], F32))
+            own.append(tile(f"own{t}", [P, U], F32))
+            nc.scalar.activation(other[t][:], pg[t][:], ACT.Copy, scale=half_gain[:, t : t + 1])
+            nc.scalar.activation(own[t][:], pg[t][:], ACT.Copy, scale=gain[:, t : t + 1])
+            z_piece(za, t, 0, BANK)
+
+        cb_picked = tile("cb_picked", [P, C], U8, tag="gain")
+        nc.vector.tensor_copy(out=cb_picked[:], in_=x_bytes[:].indirect(cand_t[:]))
+        cb = tile("cb", [P, C], U8)
+        deal(nc, cb[:], cb_picked[:])
+
+        zb = tile("zb", [P, PACK, 256], F32, tag="slot3")
+        for t in range(PACK):
+            z_piece(zb, t, 512, 768)
+
+        z16 = [tile("z16_0", [P, BANK, PACK], BF16), tile("z16_1", [P, BANK, PACK], BF16)]
+        zw = [tile(f"zw{u}", [P, BANK], U32) for u in range(2)]
+        zs = [tile(f"zs{u}", [P, BANK], U8) for u in range(2)]
+
+        def quantize(u):
+            nc.vector.quantize_mx(out=zw[u][:].bitcast(FP8X4), scales=zs[u][:], in_=z16[u][:].rearrange("p w t -> p (w t)"))
+
+        interleave(nc, z16[0][:], za[:])
+        quantize(0)
+        interleave(nc, z16[1][:, 0:256, :], zb[:])
+        zc = tile("zc", [P, PACK, 256], F32, tag="z16_0")
+        for t in range(PACK):
+            z_piece(zc, t, 768, 1024)
+
+        acc = {}
+        ds = [tile(f"ds{t}", [P, U], F32) for t in range(PACK)]
+
+        def score(t, u):
+            cols = slice(t * P, (t + 1) * P)
+            acc[t, u] = psum.tile([P, BANK], F32, name=f"s_acc{t}_{u}", tag=f"bank{(4 + t + 4 * u) % 8}")
+            nc.tensor.matmul_mx(acc[t, u][:], lhsT=cw[:, cols].bitcast(FP8X4), lhsT_scale=cb[:, cols],
+                                rhs=zw[u][:].bitcast(FP8X4), rhs_scale=zs[u][:], start=True, stop=True)
+
+        def send(t, u):
+            rl = tile(f"rl{t}_{u}", [P, BANK], F32)
+            nc.scalar.activation(rl[:], acc[t, u][:], ACT.Relu, scale=0.0625)
+            nc.vector.tensor_copy(out=ds[t][:].indirect(n3_t[:, 32 * u : 32 * (u + 1)]), in_=rl[:])
+
+        def finish(t):
+            for u in range(2):
+                cols = slice(u * BANK, (u + 1) * BANK)
+                res = tile(f"res{t}_{u}", [P, BANK], F32)
+                nc.vector.scalar_tensor_tensor(res[:], acc[t, u][:], -0.03125, ds[t][:, cols], ALU.mult, ALU.add)
+                nc.sync.dma_start(out_rows[t][:, cols], res[:])
+
+        for t in range(PACK):
+            score(t, 0)
+        send(0, 0)
+        interleave(nc, z16[1][:, 256:512, :], zc[:])
+        quantize(1)
+        send(1, 0)
+        for t in range(PACK):
+            score(t, 1)
+        for t in range(PACK):
+            if t >= 2:
+                send(t, 0)
+            send(t, 1)
+            finish(t)

@@ -46,53 +46,49 @@ def tile_picked_pqcpagemsend_none_p_kernel(tc, x_words, x_scales, d_words, d_sca
         out_rows = out.rearrange("(p t) w -> t p w", t=PACK)
 
         d_bytes = tile("d_bytes", [P, G], U8)
-        x_bytes = tile("x_bytes", [P, T], U8)
-        nc.vector.memset(d_bytes[:].bitcast(I32), 0)
-        nc.gpsimd.memset(x_bytes[:].bitcast(I32), 0)
+        nc.sync.dma_start(d_bytes[:].bitcast(I32), d_scales[0].bitcast(I32).unsqueeze(1).to_broadcast([16, 8, G // 4]))
+        k1_t = load_list("k1_t", k1)
         offs_t = load_list("offs_t", offs)
         x_tab = tile("x_tab", [P, T], U32)
         nc.sync.dma_start(x_tab[:].bitcast(I32), x_words[0].rearrange("p n t -> p (n t)").bitcast(I32))
-        k1_t = load_list("k1_t", k1)
-        for j in range(2):
-            nc.scalar.dma_start(d_bytes[j:P:16, :].bitcast(I32), d_scales[0, j:16:2, :].bitcast(I32))
-        cand_t = load_list("cand_t", cand)
-        n1_t = load_list("n1_t", n1)
+        x_bytes = tile("x_bytes", [P, T], U8)
+        for q in range(4):
+            nc.sync.dma_start(x_bytes[32 * q : 32 * (q + 1), :].bitcast(I32),
+                              x_scales[0, 4 * q : 4 * q + 4, :].bitcast(I32).unsqueeze(0).to_broadcast([8, 4, T // 4]))
         d_tab = tile("d_tab", [P, G], U32)
         nc.sync.dma_start(d_tab[:].bitcast(I32), d_words[0].rearrange("p n t -> p (n t)").bitcast(I32))
-        for q in range(4):
-            nc.sync.dma_start(x_bytes[32 * q : 32 * q + 4, :].bitcast(I32), x_scales[0, 4 * q : 4 * q + 4, :].bitcast(I32))
-        pg = [tile("pg0", [P, U], F32)]
-        nc.sync.dma_start(pg[0][:], mem_rows[0])
-        gain = tile("gain", [P, PACK], F32)
-        nc.sync.dma_start(gain[:], gs.rearrange("(p t) o -> p (t o)", t=PACK))
+        cand_t = load_list("cand_t", cand)
+        n1_t = load_list("n1_t", n1)
         n2_t = load_list("n2_t", n2)
         n3_t = load_list("n3_t", n3)
+        gain = tile("gain", [P, PACK], F32)
+        nc.gpsimd.dma_start(gain[:], gs.rearrange("(p t) o -> p (t o)", t=PACK))
+        half_gain = tile("half_gain", [P, PACK], F32)
+        nc.scalar.activation(half_gain[:], gain[:], ACT.Copy, scale=-0.5)
 
-        xw = tile("xw", [P, S], U32)
-        nc.vector.tensor_copy(out=xw[:], in_=x_tab[:].indirect(offs_t[:]))
-        db_picked = tile("db_picked", [P, H], U8, tag="slot1")
+        db_picked = tile("db_picked", [P, H], U8)
         nc.vector.tensor_copy(out=db_picked[:], in_=d_bytes[:].indirect(k1_t[:]))
         db = tile("db", [P, H], U8)
         deal(nc, db[:], db_picked[:])
-        for j in range(2):
-            nc.scalar.dma_start(db[2 + j : P : 32, :].bitcast(I32), db[16 + j : P : 32, :].bitcast(I32))
-        dw_picked = tile("dw_picked", [P, H], U32, tag="slot3")
+        for j in range(1, 4):
+            nc.scalar.dma_start(db[j:P:32, :].bitcast(I32), db[8 * j : P : 32, :].bitcast(I32))
+        xw = tile("xw", [P, S], U32)
+        nc.vector.tensor_copy(out=xw[:], in_=x_tab[:].indirect(offs_t[:]))
+        xb = tile("xb", [P, S], U8)
+        nc.vector.tensor_copy(out=xb[:], in_=x_bytes[:].indirect(offs_t[:]))
+        dw_picked = tile("dw_picked", [P, H], U32)
         nc.vector.tensor_copy(out=dw_picked[:], in_=d_tab[:].indirect(k1_t[:]))
         dw = tile("dw", [P, H], U32)
         deal(nc, dw[:], dw_picked[:])
-        xb = tile("xb", [P, S], U8)
-        nc.vector.tensor_copy(out=xb[:], in_=x_bytes[:].indirect(offs_t[:]))
-        cw_picked = tile("cw_picked", [P, C], U32)
+        cw_picked = tile("cw_picked", [P, C], U32, tag="dw_picked")
         nc.vector.tensor_copy(out=cw_picked[:], in_=x_tab[:].indirect(cand_t[:]))
         cw = tile("cw", [P, C], U32)
         deal(nc, cw[:], cw_picked[:])
 
-        for t, tag in ((1, "slot1"), (2, "d_tab"), (3, "slot3")):
+        pg = []
+        for t, tag in enumerate(("db_picked", "d_tab", "x_tab", "dw_picked")):
             pg.append(tile(f"pg{t}", [P, U], F32, tag=tag))
-            nc.sync.dma_start(pg[t][:], mem_rows[t])
-
-        half_gain = tile("half_gain", [P, PACK], F32)
-        nc.scalar.activation(half_gain[:], gain[:], ACT.Copy, scale=-0.5)
+            (nc.scalar if t == 0 else nc.sync).dma_start(pg[t][:], mem_rows[t])
 
         for t in range(PACK):
             cols = slice(t * P, (t + 1) * P)
@@ -121,7 +117,7 @@ def tile_picked_pqcpagemsend_none_p_kernel(tc, x_words, x_scales, d_words, d_sca
         cb = tile("cb", [P, C], U8)
         deal(nc, cb[:], cb_picked[:])
 
-        zb = tile("zb", [P, PACK, 256], F32, tag="slot3")
+        zb = tile("zb", [P, PACK, 256], F32, tag="dw_picked")
         for t in range(PACK):
             z_piece(zb, t, 512, 768)
 
@@ -157,7 +153,12 @@ def tile_picked_pqcpagemsend_none_p_kernel(tc, x_words, x_scales, d_words, d_sca
             for u in range(2):
                 cols = slice(u * BANK, (u + 1) * BANK)
                 res = tile(f"res{t}_{u}", [P, BANK], F32)
-                nc.vector.scalar_tensor_tensor(res[:], acc[t, u][:], -0.03125, ds[t][:, cols], ALU.mult, ALU.add)
+                if t == PACK - 1:
+                    nc.vector.scalar_tensor_tensor(res[:], acc[t, u][:], -0.03125, ds[t][:, cols], ALU.mult, ALU.add)
+                else:
+                    less = tile(f"less{t}_{u}", [P, BANK], F32)
+                    nc.scalar.activation(less[:], acc[t, u][:], ACT.Copy, scale=-0.03125)
+                    nc.gpsimd.tensor_tensor(res[:], less[:], ds[t][:, cols], ALU.add)
                 nc.sync.dma_start(out_rows[t][:, cols], res[:])
 
         for t in range(PACK):

@@ -43,7 +43,7 @@ def tile_picked_pqcpagemsend_none_p_kernel(tc, x_words, x_scales, d_words, d_sca
             return t
 
         mem_rows = mem.rearrange("(p t) w -> t p w", t=PACK)
-        out_rows = out.rearrange("(p t) w -> t p w", t=PACK)
+        out_rows = out.rearrange("(a t i) w -> t a i w", t=PACK, i=4)
 
         d_bytes = tile("d_bytes", [P, G], U8)
         nc.sync.dma_start(d_bytes[:].bitcast(I32), d_scales[0].bitcast(I32).unsqueeze(1).to_broadcast([16, 8, G // 4]))
@@ -72,6 +72,8 @@ def tile_picked_pqcpagemsend_none_p_kernel(tc, x_words, x_scales, d_words, d_sca
         deal(nc, db[:], db_picked[:])
         for j in range(1, 4):
             nc.scalar.dma_start(db[j:P:32, :].bitcast(I32), db[8 * j : P : 32, :].bitcast(I32))
+        pg0 = tile("pg0", [P, U], F32, tag="db_picked")
+        nc.scalar.dma_start(pg0[:], mem_rows[0])
         xw = tile("xw", [P, S], U32)
         nc.vector.tensor_copy(out=xw[:], in_=x_tab[:].indirect(offs_t[:]))
         xb = tile("xb", [P, S], U8)
@@ -79,25 +81,28 @@ def tile_picked_pqcpagemsend_none_p_kernel(tc, x_words, x_scales, d_words, d_sca
         dw_picked = tile("dw_picked", [P, H], U32)
         nc.vector.tensor_copy(out=dw_picked[:], in_=d_tab[:].indirect(k1_t[:]))
         dw = tile("dw", [P, H], U32)
-        deal(nc, dw[:], dw_picked[:])
-        cw_picked = tile("cw_picked", [P, C], U32, tag="dw_picked")
-        nc.vector.tensor_copy(out=cw_picked[:], in_=x_tab[:].indirect(cand_t[:]))
-        cw = tile("cw", [P, C], U32)
-        deal(nc, cw[:], cw_picked[:])
+        dw_out = dw[:].rearrange("p (t c i) -> p c t i", t=PACK, i=4)
+        dw_in = dw_picked[:].rearrange("p (c i t) -> p c t i", t=PACK, i=4)
+        nc.vector.tensor_copy(out=dw_out[:, :, 0:1, :], in_=dw_in[:, :, 0:1, :])
+        nc.vector.tensor_copy(out=dw_out[:, :, 1:PACK, :], in_=dw_in[:, :, 1:PACK, :])
+        cw = tile("cw", [P, C], U32, tag="dw_picked")
+        nc.vector.tensor_copy(out=cw[:].rearrange("p (t a i) -> p a t i", t=PACK, i=4), in_=x_tab[:].indirect(cand_t[:]))
 
-        pg = []
-        for t, tag in enumerate(("db_picked", "d_tab", "x_tab", "dw_picked")):
-            pg.append(tile(f"pg{t}", [P, U], F32, tag=tag))
-            (nc.scalar if t == 0 else nc.sync).dma_start(pg[t][:], mem_rows[t])
+        h = []
 
         for t in range(PACK):
             cols = slice(t * P, (t + 1) * P)
             acc = psum.tile([P, S], F32, name=f"h_acc{t}", tag=f"bank{t}")
             nc.tensor.matmul_mx(acc[:], lhsT=dw[:, cols].bitcast(FP8X4), lhsT_scale=db[:, cols],
                                 rhs=xw[:].bitcast(FP8X4), rhs_scale=xb[:], start=True, stop=True)
-            h = tile(f"h{t}", [P, S], F32)
-            nc.scalar.activation(h[:], acc[:], ACT.Copy, scale=0.0625)
-            nc.vector.tensor_copy(out=pg[t][:].indirect(n1_t[:]), in_=h[:])
+            h.append(tile(f"h{t}", [P, S], F32))
+            nc.scalar.activation(h[t][:], acc[:], ACT.Copy, scale=0.0625)
+        pg = [pg0]
+        for t, tag in ((1, "d_tab"), (2, "x_tab"), (3, "xw")):
+            pg.append(tile(f"pg{t}", [P, U], F32, tag=tag))
+            nc.sync.dma_start(pg[t][:], mem_rows[t])
+        for t in range(PACK):
+            nc.vector.tensor_copy(out=pg[t][:].indirect(n1_t[:]), in_=h[t][:])
 
         own, other = [], []
         za = tile("za", [P, PACK, BANK], F32)
@@ -115,9 +120,10 @@ def tile_picked_pqcpagemsend_none_p_kernel(tc, x_words, x_scales, d_words, d_sca
         cb_picked = tile("cb_picked", [P, C], U8, tag="gain")
         nc.vector.tensor_copy(out=cb_picked[:], in_=x_bytes[:].indirect(cand_t[:]))
         cb = tile("cb", [P, C], U8)
-        deal(nc, cb[:], cb_picked[:])
+        nc.vector.tensor_copy(out=cb[:].bitcast(I32).rearrange("p (t a) -> p t a", t=PACK),
+                              in_=cb_picked[:].bitcast(I32).rearrange("p (a t) -> p t a", t=PACK))
 
-        zb = tile("zb", [P, PACK, 256], F32, tag="dw_picked")
+        zb = tile("zb", [P, PACK, 256], F32, tag="xw")
         for t in range(PACK):
             z_piece(zb, t, 512, 768)
 
@@ -136,7 +142,8 @@ def tile_picked_pqcpagemsend_none_p_kernel(tc, x_words, x_scales, d_words, d_sca
             z_piece(zc, t, 768, 1024)
 
         acc = {}
-        ds = [tile(f"ds{t}", [P, U], F32) for t in range(PACK)]
+        ds = [tile(f"ds{t}", [P, U if t < 2 else 2 * U], F32) for t in range(PACK)]
+        rl = {}
 
         def score(t, u):
             cols = slice(t * P, (t + 1) * P)
@@ -144,33 +151,48 @@ def tile_picked_pqcpagemsend_none_p_kernel(tc, x_words, x_scales, d_words, d_sca
             nc.tensor.matmul_mx(acc[t, u][:], lhsT=cw[:, cols].bitcast(FP8X4), lhsT_scale=cb[:, cols],
                                 rhs=zw[u][:].bitcast(FP8X4), rhs_scale=zs[u][:], start=True, stop=True)
 
-        def send(t, u):
-            rl = tile(f"rl{t}_{u}", [P, BANK], F32)
-            nc.scalar.activation(rl[:], acc[t, u][:], ACT.Relu, scale=0.0625)
-            nc.vector.tensor_copy(out=ds[t][:].indirect(n3_t[:, 32 * u : 32 * (u + 1)]), in_=rl[:])
+        def send(t, halves):
+            if t not in rl:
+                rl[t] = tile(f"rl{t}", [P, U], F32, tag="z16_0" if t == 1 else None)
+            for u in halves:
+                nc.scalar.activation(rl[t][:, u * BANK : (u + 1) * BANK], acc[t, u][:], ACT.Relu, scale=0.0625)
+            w0, w1 = halves[0] * BANK, (halves[-1] + 1) * BANK
+            nc.vector.tensor_copy(out=ds[t][:].indirect(n3_t[:, w0 // 16 : w1 // 16]), in_=rl[t][:, w0:w1])
 
         def finish(t):
             for u in range(2):
                 cols = slice(u * BANK, (u + 1) * BANK)
                 res = tile(f"res{t}_{u}", [P, BANK], F32)
-                if t == PACK - 1:
-                    nc.vector.scalar_tensor_tensor(res[:], acc[t, u][:], -0.03125, ds[t][:, cols], ALU.mult, ALU.add)
-                else:
-                    less = tile(f"less{t}_{u}", [P, BANK], F32)
-                    nc.scalar.activation(less[:], acc[t, u][:], ACT.Copy, scale=-0.03125)
+                less = tile(f"less{t}_{u}", [P, BANK], F32)
+                nc.scalar.activation(less[:], acc[t, u][:], ACT.Copy, scale=-0.03125)
+                nc.gpsimd.tensor_tensor(res[:], less[:], ds[t][:, cols], ALU.add)
+                nc.sync.dma_start(out_rows[t][:, :, cols], res[:])
+
+        def finish_last(t):
+            for v in range(4):
+                u, c0 = divmod(v * 256, BANK)
+                cols = slice(v * 256, (v + 1) * 256)
+                res = tile(f"res{t}_{v}", [P, 256], F32)
+                if v == 1:
+                    less = tile(f"less{t}", [P, 256], F32)
+                    nc.scalar.activation(less[:], acc[t, u][:, c0 : c0 + 256], ACT.Copy, scale=-0.03125)
                     nc.gpsimd.tensor_tensor(res[:], less[:], ds[t][:, cols], ALU.add)
-                nc.sync.dma_start(out_rows[t][:, cols], res[:])
+                else:
+                    nc.vector.scalar_tensor_tensor(res[:], acc[t, u][:, c0 : c0 + 256], -0.03125, ds[t][:, cols], ALU.mult, ALU.add)
+                (nc.sync if v % 2 == 0 else nc.scalar).dma_start(out_rows[t][:, :, cols], res[:])
 
         for t in range(PACK):
             score(t, 0)
-        send(0, 0)
+        send(0, [0])
         interleave(nc, z16[1][:, 256:512, :], zc[:])
         quantize(1)
-        send(1, 0)
+        send(1, [0])
         for t in range(PACK):
             score(t, 1)
-        for t in range(PACK):
-            if t >= 2:
-                send(t, 0)
-            send(t, 1)
+        for t in range(2):
+            send(t, [1])
             finish(t)
+        send(2, [0, 1])
+        finish(2)
+        send(3, [0, 1])
+        finish_last(3)

@@ -14,178 +14,192 @@ ACT = mybir.ActivationFunctionType
 
 P = 128
 PACK = 4
+GROUP = 16
+QUAD = 32
 K, T, S, G, H, U, C = 512, 1024, 512, 2048, 512, 1024, 512
-BANK = 512
+HALF = U // 2
+QUARTER = U // 4
+LAST = PACK - 1
 FLOPS = 2 * K * H * S + 2 * K * C * U
 
 
-def deal(nc, out, in_):
-    nc.vector.tensor_copy(out=out.rearrange("p (t m) -> p t m", t=PACK), in_=in_.rearrange("p (m t) -> p t m", t=PACK))
-
-
-def interleave(nc, out, in_):
-    nc.scalar.copy(out=out.rearrange("p (c i) t -> p c t i", i=4), in_=in_.rearrange("p t (c i) -> p c t i", i=4))
-
-
-def tile_picked_pqcpagemsend_none_p_kernel(tc, x_words, x_scales, d_words, d_scales, mem, gs, offs, k1, n1, n2, cand, n3, out):
+def tile_picked_pqcpagemsend_none_p_kernel(
+    tc, x_words, x_scales, d_words, d_scales, mem, gs, offs, k1, n1, n2, cand, n3, out
+):
     nc = tc.nc
     with ExitStack() as ctx:
         lists = ctx.enter_context(tc.tile_pool(name="lists", bufs=1))
         sb = ctx.enter_context(tc.tile_pool(name="sb", bufs=1))
         psum = ctx.enter_context(tc.psum_pool(name="psum", bufs=1))
 
-        def tile(name, shape, dtype, tag=None):
-            return sb.tile(shape, dtype, name=name, tag=tag or name, align_bytes=64)
+        def tile(name, shape, dtype, after=None):
+            return sb.tile(shape, dtype, name=name, tag=after or name, align_bytes=64)
 
         def load_list(name, src):
-            t = lists.tile(list(src.shape), U16, name=name)
-            nc.sync.dma_start(t[:], src)
-            return t
+            offsets = lists.tile(list(src.shape), U16, name=name)
+            nc.sync.dma_start(offsets[:], src)
+            return offsets
+
+        def entries(offsets, first, end):
+            return offsets[:, first // GROUP : end // GROUP]
+
+        def half(u):
+            return slice(u * HALF, (u + 1) * HALF)
 
         mem_rows = mem.rearrange("(p t) w -> t p w", t=PACK)
-        out_rows = out.rearrange("(a t i) w -> t a i w", t=PACK, i=4)
+        out_rows = out.rearrange("(a t i) w -> t a i w", t=PACK, i=PACK)
 
         d_bytes = tile("d_bytes", [P, G], U8)
-        nc.sync.dma_start(d_bytes[:].bitcast(I32), d_scales[0].bitcast(I32).unsqueeze(1).to_broadcast([16, 8, G // 4]))
-        k1_t = load_list("k1_t", k1)
-        offs_t = load_list("offs_t", offs)
-        x_tab = tile("x_tab", [P, T], U32)
-        nc.sync.dma_start(x_tab[:].bitcast(I32), x_words[0].rearrange("p n t -> p (n t)").bitcast(I32))
+        nc.sync.dma_start(d_bytes[:].bitcast(I32), d_scales[0].bitcast(I32).unsqueeze(1).to_broadcast([16, 8, G // PACK]))
+        k1_list = load_list("k1_list", k1)
+        offs_list = load_list("offs_list", offs)
+        x_table = tile("x_table", [P, T], U32)
+        nc.sync.dma_start(x_table[:].bitcast(I32), x_words[0].rearrange("p n t -> p (n t)").bitcast(I32))
         x_bytes = tile("x_bytes", [P, T], U8)
-        for q in range(4):
-            nc.sync.dma_start(x_bytes[32 * q : 32 * (q + 1), :].bitcast(I32),
-                              x_scales[0, 4 * q : 4 * q + 4, :].bitcast(I32).unsqueeze(0).to_broadcast([8, 4, T // 4]))
-        d_tab = tile("d_tab", [P, G], U32)
-        nc.sync.dma_start(d_tab[:].bitcast(I32), d_words[0].rearrange("p n t -> p (n t)").bitcast(I32))
-        cand_t = load_list("cand_t", cand)
-        n1_t = load_list("n1_t", n1)
-        n2_t = load_list("n2_t", n2)
-        n3_t = load_list("n3_t", n3)
+        for q in range(P // QUAD):
+            rows = x_scales[0, 4 * q : 4 * q + 4, :].bitcast(I32)
+            nc.sync.dma_start(
+                x_bytes[QUAD * q : QUAD * (q + 1), :].bitcast(I32), rows.unsqueeze(0).to_broadcast([8, 4, T // PACK])
+            )
+        d_table = tile("d_table", [P, G], U32)
+        nc.sync.dma_start(d_table[:].bitcast(I32), d_words[0].rearrange("p n t -> p (n t)").bitcast(I32))
+        cand_list = load_list("cand_list", cand)
+        n1_list = load_list("n1_list", n1)
+        n2_list = load_list("n2_list", n2)
+        n3_list = load_list("n3_list", n3)
         gain = tile("gain", [P, PACK], F32)
         nc.gpsimd.dma_start(gain[:], gs.rearrange("(p t) o -> p (t o)", t=PACK))
         half_gain = tile("half_gain", [P, PACK], F32)
         nc.scalar.activation(half_gain[:], gain[:], ACT.Copy, scale=-0.5)
 
         db_picked = tile("db_picked", [P, H], U8)
-        nc.vector.tensor_copy(out=db_picked[:], in_=d_bytes[:].indirect(k1_t[:]))
+        nc.vector.tensor_copy(out=db_picked[:], in_=d_bytes[:].indirect(k1_list[:]))
         db = tile("db", [P, H], U8)
-        deal(nc, db[:], db_picked[:])
+        nc.vector.tensor_copy(
+            out=db[:].rearrange("p (t m) -> p t m", t=PACK), in_=db_picked[:].rearrange("p (m t) -> p t m", t=PACK)
+        )
         for j in range(1, 4):
-            nc.scalar.dma_start(db[j:P:32, :].bitcast(I32), db[8 * j : P : 32, :].bitcast(I32))
-        pg0 = tile("pg0", [P, U], F32, tag="db_picked")
-        nc.scalar.dma_start(pg0[:], mem_rows[0])
+            nc.scalar.dma_start(db[j:P:QUAD, :].bitcast(I32), db[8 * j : P : QUAD, :].bitcast(I32))
+        pg = [tile("pg0", [P, U], F32, after="db_picked")]
+        nc.scalar.dma_start(pg[0][:], mem_rows[0])
+
         xw = tile("xw", [P, S], U32)
-        nc.vector.tensor_copy(out=xw[:], in_=x_tab[:].indirect(offs_t[:]))
+        nc.vector.tensor_copy(out=xw[:], in_=x_table[:].indirect(offs_list[:]))
         xb = tile("xb", [P, S], U8)
-        nc.vector.tensor_copy(out=xb[:], in_=x_bytes[:].indirect(offs_t[:]))
+        nc.vector.tensor_copy(out=xb[:], in_=x_bytes[:].indirect(offs_list[:]))
         dw_picked = tile("dw_picked", [P, H], U32)
-        nc.vector.tensor_copy(out=dw_picked[:], in_=d_tab[:].indirect(k1_t[:]))
+        nc.vector.tensor_copy(out=dw_picked[:], in_=d_table[:].indirect(k1_list[:]))
         dw = tile("dw", [P, H], U32)
         dw_out = dw[:].rearrange("p (t c i) -> p c t i", t=PACK, i=4)
         dw_in = dw_picked[:].rearrange("p (c i t) -> p c t i", t=PACK, i=4)
         nc.vector.tensor_copy(out=dw_out[:, :, 0:1, :], in_=dw_in[:, :, 0:1, :])
         nc.vector.tensor_copy(out=dw_out[:, :, 1:PACK, :], in_=dw_in[:, :, 1:PACK, :])
-        cw = tile("cw", [P, C], U32, tag="dw_picked")
-        nc.vector.tensor_copy(out=cw[:].rearrange("p (t a i) -> p a t i", t=PACK, i=4), in_=x_tab[:].indirect(cand_t[:]))
+        cw = tile("cw", [P, C], U32, after="dw_picked")
+        nc.vector.tensor_copy(
+            out=cw[:].rearrange("p (t a i) -> p a t i", t=PACK, i=PACK), in_=x_table[:].indirect(cand_list[:])
+        )
 
         h = []
-
         for t in range(PACK):
             cols = slice(t * P, (t + 1) * P)
-            acc = psum.tile([P, S], F32, name=f"h_acc{t}", tag=f"bank{t}")
-            nc.tensor.matmul_mx(acc[:], lhsT=dw[:, cols].bitcast(FP8X4), lhsT_scale=db[:, cols],
-                                rhs=xw[:].bitcast(FP8X4), rhs_scale=xb[:], start=True, stop=True)
+            h_acc = psum.tile([P, S], F32, name=f"h_acc{t}", tag=f"bank{t}")
+            nc.tensor.matmul_mx(
+                h_acc[:], lhsT=dw[:, cols].bitcast(FP8X4), lhsT_scale=db[:, cols],
+                rhs=xw[:].bitcast(FP8X4), rhs_scale=xb[:], start=True, stop=True,
+            )
             h.append(tile(f"h{t}", [P, S], F32))
-            nc.scalar.activation(h[t][:], acc[:], ACT.Copy, scale=0.0625)
-        pg = [pg0]
-        for t, tag in ((1, "d_tab"), (2, "x_tab"), (3, "xw")):
-            pg.append(tile(f"pg{t}", [P, U], F32, tag=tag))
+            nc.scalar.activation(h[t][:], h_acc[:], ACT.Copy, scale=0.0625)
+        for t, spent in ((1, "d_table"), (2, "x_table"), (3, "xw")):
+            pg.append(tile(f"pg{t}", [P, U], F32, after=spent))
             nc.sync.dma_start(pg[t][:], mem_rows[t])
         for t in range(PACK):
-            nc.vector.tensor_copy(out=pg[t][:].indirect(n1_t[:]), in_=h[t][:])
+            nc.vector.tensor_copy(out=pg[t][:].indirect(n1_list[:]), in_=h[t][:])
 
-        own, other = [], []
-        za = tile("za", [P, PACK, BANK], F32)
+        other = [tile(f"other{t}", [P, U], F32) for t in range(PACK)]
+        z = [tile("z0", [P, PACK, HALF], F32)]
 
-        def z_piece(dst, t, w0, w1):
-            nc.vector.tensor_tensor(dst[:, t, :], other[t][:].indirect(n2_t[:, w0 // 16 : w1 // 16]), own[t][:, w0:w1], ALU.add)
+        def scale_own(own, t, u):
+            nc.scalar.activation(own, pg[t][:, half(u)], ACT.Copy, scale=gain[:, t : t + 1])
 
+        def z_half(t, u, own):
+            looked_up = other[t][:].indirect(entries(n2_list, u * HALF, (u + 1) * HALF))
+            nc.vector.tensor_tensor(z[u][:, t, :], looked_up, own, ALU.add)
+
+        own_second = []
         for t in range(PACK):
-            other.append(tile(f"other{t}", [P, U], F32))
-            own.append(tile(f"own{t}", [P, U], F32))
+            own_first = tile(f"own{t}_0", [P, HALF], F32)
+            scale_own(own_first[:], t, 0)
             nc.scalar.activation(other[t][:], pg[t][:], ACT.Copy, scale=half_gain[:, t : t + 1])
-            nc.scalar.activation(own[t][:], pg[t][:], ACT.Copy, scale=gain[:, t : t + 1])
-            z_piece(za, t, 0, BANK)
+            z_half(t, 0, own_first[:])
+            if t < 2:
+                own_second.append(tile(f"own{t}_1", [P, HALF], F32))
+                scale_own(own_second[t][:], t, 1)
 
-        cb_picked = tile("cb_picked", [P, C], U8, tag="gain")
-        nc.vector.tensor_copy(out=cb_picked[:], in_=x_bytes[:].indirect(cand_t[:]))
+        cb_picked = tile("cb_picked", [P, C], U8, after=f"own{LAST}_0")
+        nc.vector.tensor_copy(out=cb_picked[:], in_=x_bytes[:].indirect(cand_list[:]))
+        z.append(tile("z1", [P, PACK, HALF], F32, after="half_gain"))
+        z_half(0, 1, own_second[0][:])
         cb = tile("cb", [P, C], U8)
-        nc.vector.tensor_copy(out=cb[:].bitcast(I32).rearrange("p (t a) -> p t a", t=PACK),
-                              in_=cb_picked[:].bitcast(I32).rearrange("p (a t) -> p t a", t=PACK))
+        nc.vector.tensor_copy(
+            out=cb[:].bitcast(I32).rearrange("p (t a) -> p t a", t=PACK),
+            in_=cb_picked[:].bitcast(I32).rearrange("p (a t) -> p t a", t=PACK),
+        )
+        z_half(1, 1, own_second[1][:])
 
-        zb = tile("zb", [P, PACK, 256], F32, tag="xw")
-        for t in range(PACK):
-            z_piece(zb, t, 512, 768)
+        z16 = [tile(f"z16_{u}", [P, HALF, PACK], BF16) for u in range(2)]
+        zw = [tile(f"zw{u}", [P, HALF], U32) for u in range(2)]
+        zb = [tile(f"zb{u}", [P, HALF], U8) for u in range(2)]
 
-        z16 = [tile("z16_0", [P, BANK, PACK], BF16), tile("z16_1", [P, BANK, PACK], BF16)]
-        zw = [tile(f"zw{u}", [P, BANK], U32) for u in range(2)]
-        zs = [tile(f"zs{u}", [P, BANK], U8) for u in range(2)]
+        def round_and_quantize(u):
+            nc.scalar.copy(
+                out=z16[u][:].rearrange("p (c i) t -> p c t i", i=4), in_=z[u][:].rearrange("p t (c i) -> p c t i", i=4)
+            )
+            nc.vector.quantize_mx(
+                out=zw[u][:].bitcast(FP8X4), scales=zb[u][:], in_=z16[u][:].rearrange("p w t -> p (w t)")
+            )
 
-        def quantize(u):
-            nc.vector.quantize_mx(out=zw[u][:].bitcast(FP8X4), scales=zs[u][:], in_=z16[u][:].rearrange("p w t -> p (w t)"))
+        round_and_quantize(0)
+        own_held = tile("own_held", [P, 2, HALF], F32, after="z0")
+        for t in (2, 3):
+            scale_own(own_held[:, t - 2, :], t, 1)
+            z_half(t, 1, own_held[:, t - 2, :])
 
-        interleave(nc, z16[0][:], za[:])
-        quantize(0)
-        interleave(nc, z16[1][:, 0:256, :], zb[:])
-        zc = tile("zc", [P, PACK, 256], F32, tag="z16_0")
-        for t in range(PACK):
-            z_piece(zc, t, 768, 1024)
-
-        acc = {}
+        s_acc = {}
         ds = [tile(f"ds{t}", [P, U if t < 2 else 2 * U], F32) for t in range(PACK)]
         rl = {}
 
         def score(t, u):
             cols = slice(t * P, (t + 1) * P)
-            acc[t, u] = psum.tile([P, BANK], F32, name=f"s_acc{t}_{u}", tag=f"bank{(4 + t + 4 * u) % 8}")
-            nc.tensor.matmul_mx(acc[t, u][:], lhsT=cw[:, cols].bitcast(FP8X4), lhsT_scale=cb[:, cols],
-                                rhs=zw[u][:].bitcast(FP8X4), rhs_scale=zs[u][:], start=True, stop=True)
+            s_acc[t, u] = psum.tile([P, HALF], F32, name=f"s_acc{t}_{u}", tag=f"bank{t + PACK * (1 - u)}")
+            nc.tensor.matmul_mx(
+                s_acc[t, u][:], lhsT=cw[:, cols].bitcast(FP8X4), lhsT_scale=cb[:, cols],
+                rhs=zw[u][:].bitcast(FP8X4), rhs_scale=zb[u][:], start=True, stop=True,
+            )
 
         def send(t, halves):
             if t not in rl:
-                rl[t] = tile(f"rl{t}", [P, U], F32, tag="z16_0" if t == 1 else None)
+                rl[t] = tile(f"rl{t}", [P, U], F32, after="half_gain" if t == 1 else None)
             for u in halves:
-                nc.scalar.activation(rl[t][:, u * BANK : (u + 1) * BANK], acc[t, u][:], ACT.Relu, scale=0.0625)
-            w0, w1 = halves[0] * BANK, (halves[-1] + 1) * BANK
-            nc.vector.tensor_copy(out=ds[t][:].indirect(n3_t[:, w0 // 16 : w1 // 16]), in_=rl[t][:, w0:w1])
+                nc.scalar.activation(rl[t][:, half(u)], s_acc[t, u][:], ACT.Relu, scale=0.0625)
+            first, end = halves[0] * HALF, (halves[-1] + 1) * HALF
+            nc.vector.tensor_copy(out=ds[t][:].indirect(entries(n3_list, first, end)), in_=rl[t][:, first:end])
+
+        def minus_half_s(name, bank_cols):
+            less = tile(name, list(bank_cols.shape), F32)
+            nc.scalar.activation(less[:], bank_cols, ACT.Copy, scale=-0.5 * 0.0625)
+            return less
 
         def finish(t):
             for u in range(2):
-                cols = slice(u * BANK, (u + 1) * BANK)
-                res = tile(f"res{t}_{u}", [P, BANK], F32)
-                less = tile(f"less{t}_{u}", [P, BANK], F32)
-                nc.scalar.activation(less[:], acc[t, u][:], ACT.Copy, scale=-0.03125)
-                nc.gpsimd.tensor_tensor(res[:], less[:], ds[t][:, cols], ALU.add)
-                nc.sync.dma_start(out_rows[t][:, :, cols], res[:])
-
-        def finish_last(t):
-            for v in range(4):
-                u, c0 = divmod(v * 256, BANK)
-                cols = slice(v * 256, (v + 1) * 256)
-                res = tile(f"res{t}_{v}", [P, 256], F32)
-                if v == 1:
-                    less = tile(f"less{t}", [P, 256], F32)
-                    nc.scalar.activation(less[:], acc[t, u][:, c0 : c0 + 256], ACT.Copy, scale=-0.03125)
-                    nc.gpsimd.tensor_tensor(res[:], less[:], ds[t][:, cols], ALU.add)
-                else:
-                    nc.vector.scalar_tensor_tensor(res[:], acc[t, u][:, c0 : c0 + 256], -0.03125, ds[t][:, cols], ALU.mult, ALU.add)
-                (nc.sync if v % 2 == 0 else nc.scalar).dma_start(out_rows[t][:, :, cols], res[:])
+                res = tile(f"res{t}_{u}", [P, HALF], F32)
+                less = minus_half_s(f"less{t}_{u}", s_acc[t, u][:])
+                nc.gpsimd.tensor_tensor(res[:], less[:], ds[t][:, half(u)], ALU.add)
+                nc.sync.dma_start(out_rows[t][:, :, half(u)], res[:])
 
         for t in range(PACK):
             score(t, 0)
         send(0, [0])
-        interleave(nc, z16[1][:, 256:512, :], zc[:])
-        quantize(1)
+        round_and_quantize(1)
         send(1, [0])
         for t in range(PACK):
             score(t, 1)
@@ -194,5 +208,16 @@ def tile_picked_pqcpagemsend_none_p_kernel(tc, x_words, x_scales, d_words, d_sca
             finish(t)
         send(2, [0, 1])
         finish(2)
-        send(3, [0, 1])
-        finish_last(3)
+        send(LAST, [0, 1])
+
+        less_second = minus_half_s("less_second", s_acc[LAST, 0][:, QUARTER:HALF])
+        for v in range(U // QUARTER):
+            u, first = divmod(v * QUARTER, HALF)
+            cols = slice(v * QUARTER, (v + 1) * QUARTER)
+            res = tile(f"res{LAST}_{v}", [P, QUARTER], F32)
+            if v == 1:
+                nc.gpsimd.tensor_tensor(res[:], less_second[:], ds[LAST][:, cols], ALU.add)
+            else:
+                bank_cols = s_acc[LAST, u][:, first : first + QUARTER]
+                nc.vector.scalar_tensor_tensor(res[:], bank_cols, -0.5 * 0.0625, ds[LAST][:, cols], ALU.mult, ALU.add)
+            (nc.sync if v % 2 == 0 else nc.scalar).dma_start(out_rows[LAST][:, :, cols], res[:])

from contextlib import ExitStack

import concourse.mybir as mybir

F32 = mybir.dt.float32
BF16 = mybir.dt.bfloat16
I32 = mybir.dt.int32
U32 = mybir.dt.uint32
U16 = mybir.dt.uint16
U8 = mybir.dt.uint8
FP8X4 = mybir.dt.float8_e4m3fn_x4
ALU = mybir.AluOpType
ACT = mybir.ActivationFunctionType

P = 128
PACK = 4
GROUP = 16
QUAD = 32
K, T, S, G, H, U, C = 512, 1024, 512, 2048, 512, 1024, 512
HALF = U // 2
QUARTER = U // 4
LAST = PACK - 1
FLOPS = 2 * K * H * S + 2 * K * C * U


def tile_picked_pqcpagemsend_none_p_kernel(
    tc, x_words, x_scales, d_words, d_scales, mem, gs, offs, k1, n1, n2, cand, n3, out
):
    nc = tc.nc
    with ExitStack() as ctx:
        lists = ctx.enter_context(tc.tile_pool(name="lists", bufs=1))
        sb = ctx.enter_context(tc.tile_pool(name="sb", bufs=1))
        psum = ctx.enter_context(tc.psum_pool(name="psum", bufs=1))

        def tile(name, shape, dtype, after=None):
            return sb.tile(shape, dtype, name=name, tag=after or name, align_bytes=64)

        def load_list(name, src):
            offsets = lists.tile(list(src.shape), U16, name=name)
            nc.sync.dma_start(offsets[:], src)
            return offsets

        def entries(offsets, first, end):
            return offsets[:, first // GROUP : end // GROUP]

        def half(u):
            return slice(u * HALF, (u + 1) * HALF)

        mem_rows = mem.rearrange("(p t) w -> t p w", t=PACK)
        out_rows = out.rearrange("(a t i) w -> t a i w", t=PACK, i=PACK)

        d_bytes = tile("d_bytes", [P, G], U8)
        nc.sync.dma_start(d_bytes[:].bitcast(I32), d_scales[0].bitcast(I32).unsqueeze(1).to_broadcast([16, 8, G // PACK]))
        k1_list = load_list("k1_list", k1)
        offs_list = load_list("offs_list", offs)
        x_table = tile("x_table", [P, T], U32)
        nc.sync.dma_start(x_table[:].bitcast(I32), x_words[0].rearrange("p n t -> p (n t)").bitcast(I32))
        x_bytes = tile("x_bytes", [P, T], U8)
        for q in range(P // QUAD):
            rows = x_scales[0, 4 * q : 4 * q + 4, :].bitcast(I32)
            nc.sync.dma_start(
                x_bytes[QUAD * q : QUAD * (q + 1), :].bitcast(I32), rows.unsqueeze(0).to_broadcast([8, 4, T // PACK])
            )
        d_table = tile("d_table", [P, G], U32)
        nc.sync.dma_start(d_table[:].bitcast(I32), d_words[0].rearrange("p n t -> p (n t)").bitcast(I32))
        cand_list = load_list("cand_list", cand)
        n1_list = load_list("n1_list", n1)
        n2_list = load_list("n2_list", n2)
        n3_list = load_list("n3_list", n3)
        gain = tile("gain", [P, PACK], F32)
        nc.gpsimd.dma_start(gain[:], gs.rearrange("(p t) o -> p (t o)", t=PACK))
        half_gain = tile("half_gain", [P, PACK], F32)
        nc.scalar.activation(half_gain[:], gain[:], ACT.Copy, scale=-0.5)

        db_picked = tile("db_picked", [P, H], U8)
        nc.vector.tensor_copy(out=db_picked[:], in_=d_bytes[:].indirect(k1_list[:]))
        db = tile("db", [P, H], U8)
        nc.vector.tensor_copy(
            out=db[:].rearrange("p (t m) -> p t m", t=PACK), in_=db_picked[:].rearrange("p (m t) -> p t m", t=PACK)
        )
        for j in range(1, 4):
            nc.scalar.dma_start(db[j:P:QUAD, :].bitcast(I32), db[8 * j : P : QUAD, :].bitcast(I32))
        pg = [tile("pg0", [P, U], F32, after="db_picked")]
        nc.scalar.dma_start(pg[0][:], mem_rows[0])

        xw = tile("xw", [P, S], U32)
        nc.vector.tensor_copy(out=xw[:], in_=x_table[:].indirect(offs_list[:]))
        xb = tile("xb", [P, S], U8)
        nc.vector.tensor_copy(out=xb[:], in_=x_bytes[:].indirect(offs_list[:]))
        dw_picked = tile("dw_picked", [P, H], U32)
        nc.vector.tensor_copy(out=dw_picked[:], in_=d_table[:].indirect(k1_list[:]))
        dw = tile("dw", [P, H], U32)
        dw_out = dw[:].rearrange("p (t c i) -> p c t i", t=PACK, i=4)
        dw_in = dw_picked[:].rearrange("p (c i t) -> p c t i", t=PACK, i=4)
        nc.vector.tensor_copy(out=dw_out[:, :, 0:1, :], in_=dw_in[:, :, 0:1, :])
        nc.vector.tensor_copy(out=dw_out[:, :, 1:PACK, :], in_=dw_in[:, :, 1:PACK, :])
        cw = tile("cw", [P, C], U32, after="dw_picked")
        nc.vector.tensor_copy(
            out=cw[:].rearrange("p (t a i) -> p a t i", t=PACK, i=PACK), in_=x_table[:].indirect(cand_list[:])
        )

        h = []
        for t in range(PACK):
            cols = slice(t * P, (t + 1) * P)
            h_acc = psum.tile([P, S], F32, name=f"h_acc{t}", tag=f"bank{t}")
            nc.tensor.matmul_mx(
                h_acc[:], lhsT=dw[:, cols].bitcast(FP8X4), lhsT_scale=db[:, cols],
                rhs=xw[:].bitcast(FP8X4), rhs_scale=xb[:], start=True, stop=True,
            )
            h.append(tile(f"h{t}", [P, S], F32))
            nc.scalar.activation(h[t][:], h_acc[:], ACT.Copy, scale=0.0625)
        for t, spent in ((1, "d_table"), (2, "x_table"), (3, "xw")):
            pg.append(tile(f"pg{t}", [P, U], F32, after=spent))
            nc.sync.dma_start(pg[t][:], mem_rows[t])
        for t in range(PACK):
            nc.vector.tensor_copy(out=pg[t][:].indirect(n1_list[:]), in_=h[t][:])

        other = [tile(f"other{t}", [P, U], F32) for t in range(PACK)]
        z = [tile("z0", [P, PACK, HALF], F32)]

        def scale_own(own, t, u):
            nc.scalar.activation(own, pg[t][:, half(u)], ACT.Copy, scale=gain[:, t : t + 1])

        def z_half(t, u, own):
            looked_up = other[t][:].indirect(entries(n2_list, u * HALF, (u + 1) * HALF))
            nc.vector.tensor_tensor(z[u][:, t, :], looked_up, own, ALU.add)

        own_second = []
        for t in range(PACK):
            own_first = tile(f"own{t}_0", [P, HALF], F32)
            scale_own(own_first[:], t, 0)
            nc.scalar.activation(other[t][:], pg[t][:], ACT.Copy, scale=half_gain[:, t : t + 1])
            z_half(t, 0, own_first[:])
            if t < 2:
                own_second.append(tile(f"own{t}_1", [P, HALF], F32))
                scale_own(own_second[t][:], t, 1)

        cb_picked = tile("cb_picked", [P, C], U8, after=f"own{LAST}_0")
        nc.vector.tensor_copy(out=cb_picked[:], in_=x_bytes[:].indirect(cand_list[:]))
        z.append(tile("z1", [P, PACK, HALF], F32, after="half_gain"))
        z_half(0, 1, own_second[0][:])
        cb = tile("cb", [P, C], U8)
        nc.vector.tensor_copy(
            out=cb[:].bitcast(I32).rearrange("p (t a) -> p t a", t=PACK),
            in_=cb_picked[:].bitcast(I32).rearrange("p (a t) -> p t a", t=PACK),
        )
        z_half(1, 1, own_second[1][:])

        z16 = [tile(f"z16_{u}", [P, HALF, PACK], BF16) for u in range(2)]
        zw = [tile(f"zw{u}", [P, HALF], U32) for u in range(2)]
        zb = [tile(f"zb{u}", [P, HALF], U8) for u in range(2)]

        def round_and_quantize(u):
            nc.scalar.copy(
                out=z16[u][:].rearrange("p (c i) t -> p c t i", i=4), in_=z[u][:].rearrange("p t (c i) -> p c t i", i=4)
            )
            nc.vector.quantize_mx(
                out=zw[u][:].bitcast(FP8X4), scales=zb[u][:], in_=z16[u][:].rearrange("p w t -> p (w t)")
            )

        round_and_quantize(0)
        own_held = tile("own_held", [P, 2, HALF], F32, after="z0")
        for t in (2, 3):
            scale_own(own_held[:, t - 2, :], t, 1)
            z_half(t, 1, own_held[:, t - 2, :])

        s_acc = {}
        ds = [tile(f"ds{t}", [P, U if t < 2 else 2 * U], F32) for t in range(PACK)]
        rl = {}

        def score(t, u):
            cols = slice(t * P, (t + 1) * P)
            s_acc[t, u] = psum.tile([P, HALF], F32, name=f"s_acc{t}_{u}", tag=f"bank{t + PACK * (1 - u)}")
            nc.tensor.matmul_mx(
                s_acc[t, u][:], lhsT=cw[:, cols].bitcast(FP8X4), lhsT_scale=cb[:, cols],
                rhs=zw[u][:].bitcast(FP8X4), rhs_scale=zb[u][:], start=True, stop=True,
            )

        def send(t, halves):
            if t not in rl:
                rl[t] = tile(f"rl{t}", [P, U], F32, after="half_gain" if t == 1 else None)
            for u in halves:
                nc.scalar.activation(rl[t][:, half(u)], s_acc[t, u][:], ACT.Relu, scale=0.0625)
            first, end = halves[0] * HALF, (halves[-1] + 1) * HALF
            nc.vector.tensor_copy(out=ds[t][:].indirect(entries(n3_list, first, end)), in_=rl[t][:, first:end])

        def minus_half_s(name, bank_cols):
            less = tile(name, list(bank_cols.shape), F32)
            nc.scalar.activation(less[:], bank_cols, ACT.Copy, scale=-0.5 * 0.0625)
            return less

        def finish(t):
            for u in range(2):
                res = tile(f"res{t}_{u}", [P, HALF], F32)
                less = minus_half_s(f"less{t}_{u}", s_acc[t, u][:])
                nc.gpsimd.tensor_tensor(res[:], less[:], ds[t][:, half(u)], ALU.add)
                nc.sync.dma_start(out_rows[t][:, :, half(u)], res[:])

        for t in range(PACK):
            score(t, 0)
        send(0, [0])
        round_and_quantize(1)
        send(1, [0])
        for t in range(PACK):
            score(t, 1)
        for t in range(2):
            send(t, [1])
            finish(t)
        send(2, [0, 1])
        finish(2)
        send(LAST, [0, 1])

        less_second = minus_half_s("less_second", s_acc[LAST, 0][:, QUARTER:HALF])
        for v in range(U // QUARTER):
            u, first = divmod(v * QUARTER, HALF)
            cols = slice(v * QUARTER, (v + 1) * QUARTER)
            res = tile(f"res{LAST}_{v}", [P, QUARTER], F32)
            if v == 1:
                nc.gpsimd.tensor_tensor(res[:], less_second[:], ds[LAST][:, cols], ALU.add)
            else:
                bank_cols = s_acc[LAST, u][:, first : first + QUARTER]
                nc.vector.scalar_tensor_tensor(res[:], bank_cols, -0.5 * 0.0625, ds[LAST][:, cols], ALU.mult, ALU.add)
            (nc.sync if v % 2 == 0 else nc.scalar).dma_start(out_rows[LAST][:, :, cols], res[:])
